import numpy as np
import ml_dtypes


def mxq(x, axis, fmt="e4m3"):
    dtype, down = {"e4m3": (ml_dtypes.float8_e4m3fn, 7), "e5m2": (ml_dtypes.float8_e5m2, 14)}[fmt]
    v = np.moveaxis(np.asarray(x, np.float32).astype(ml_dtypes.bfloat16).astype(np.float64), axis, -1)
    blocks = v.reshape(v.shape[:-1] + (-1, 32))
    amax = np.abs(blocks).max(-1, keepdims=True)
    byte = np.maximum(np.where(amax > 0, np.frexp(amax)[1] - 1 + 127, 0) - down, 1)
    scale = np.exp2(byte - 127.0)
    codes = (blocks / scale).astype(np.float32).astype(dtype).astype(np.float64)
    return np.moveaxis((codes * scale).reshape(v.shape), -1, axis)


WIDE = False


def mx_kscale(k):
    if not WIDE:
        return np.ones(k)
    levels = np.array([10, -10, 5, -5, 0])
    if k % 512:
        return np.exp2(np.random.permutation(np.resize(levels, k // 32))).repeat(32)
    a = np.empty((k // 512, 16))
    for p in range(k // 512):
        a[p, :8] = np.random.permutation(np.resize(levels, 8))
        for g in range(8):
            far = levels[np.abs(levels - a[p, g]) >= 10]
            a[p, g + 8] = far[np.random.randint(len(far))]
    return np.exp2(a.ravel()).repeat(32)


def f64(x):
    return np.asarray(x).astype(np.float64)


def striped(idx):
    return np.tile(idx.reshape(-1, 16).T, (8, 1)).astype(np.uint16)


def unstriped(offs):
    return offs[:16].T.reshape(-1).astype(np.int64)


E2M1 = np.array([0.0, 0.5, 1.0, 1.5, 2.0, 3.0, 4.0, 6.0, -0.0, -0.5, -1.0, -1.5, -2.0, -3.0, -4.0, -6.0])


def pack_weight(w, fmt):
    k, n = w.shape
    w = f64(np.asarray(w, np.float32).astype(ml_dtypes.bfloat16)).reshape(k // 32, 32, n)
    amax = np.abs(w).max(1)
    if fmt == "e4m3":
        byte = np.frexp(amax)[1] - 1 + 127 - 7
    else:
        mant, ex = np.frexp(amax / 6.0)
        byte = np.where(mant > 0.5, ex, ex - 1) + 127
    byte = np.clip(np.where(amax > 0, byte, 1), 1, 254)
    scaled = (w * np.exp2(127.0 - byte)[:, None, :]).reshape(k, n).astype(np.float32)
    by_word = np.ascontiguousarray(scaled.reshape(k // 512, 128, 4, n).transpose(0, 1, 3, 2))
    if fmt == "e4m3":
        words = by_word.astype(ml_dtypes.float8_e4m3fn).view(np.uint8)
    else:
        c = by_word.astype(ml_dtypes.float4_e2m1fn).view(np.uint8) & 0xF
        words = (c[..., 0::2] | (c[..., 1::2] << 4)).reshape(k // 512, 128, 2 * n)
    return np.ascontiguousarray(words), np.ascontiguousarray(byte.astype(np.uint8).reshape(k // 512, 16, n))


def unpack_weight(words, scales, fmt):
    g, _, n = scales.shape
    words = np.ascontiguousarray(words).reshape(g, 128, n, -1)
    if fmt == "e4m3":
        vals = words.view(ml_dtypes.float8_e4m3fn).astype(np.float64)
    else:
        nib = np.empty((g, 128, n, 4), np.uint8)
        nib[..., 0::2] = words & 0xF
        nib[..., 1::2] = words >> 4
        vals = E2M1[nib]
    vals = vals * np.repeat(np.exp2(scales.astype(np.float64) - 127.0), 8, axis=1)[..., None]
    return vals.transpose(0, 1, 3, 2).reshape(g * 512, n)


def gelu(v):
    return 0.5 * v * (1.0 + np.tanh(np.sqrt(2.0 / np.pi) * (v + 0.044715 * v**3)))


K, T, S, S2 = 1024, 2048, 512, 1024

def setup_inputs():
    n = np.random.standard_normal
    s = mx_kscale(K)[:, None]
    d = {}
    d["tab_words"], d["tab_scales"] = pack_weight(n((K, T)) * s, "e4m3")
    d["offs"] = striped(np.random.permutation(T)[:S])
    d["offs2"] = striped(np.random.permutation(T)[:S2])
    d["w4_words"], d["w4_scales"] = pack_weight(n((K, K)) / s / s.T / K, "e2m1")
    gains = np.diag(0.8 * np.exp(0.3 * n(K))) + 0.4 * n((K, K)) / K**0.5
    d["wg"] = (gains / s / s.T / K**0.5).astype(np.float32)
    d["prior"] = (0.7 * n((S2, S))).astype(np.float32)
    return d

def reference(tab_words, tab_scales, offs, offs2, w4_words, w4_scales, wg, prior):
    TW = unpack_weight(tab_words, tab_scales, "e4m3")
    v = TW[:, unstriped(offs)]
    v2 = TW[:, unstriped(offs2)]
    w4 = unpack_weight(w4_words, w4_scales, "e2m1")
    mapped = w4.T @ v
    raw = mxq(f64(wg), 0, "e4m3").T @ v
    h = np.abs(mapped - raw)
    e = v2.T @ mxq(h, 0, "e4m3")
    return np.tanh(e) + e * f64(prior)

@@ -1,0 +1,222 @@
+from contextlib import ExitStack
+
+import concourse.mybir as mybir
+
+K, T, S, S2 = 1024, 2048, 512, 1024
+FLOPS = 2 * K * K * S * 2 + 2 * K * S * S2
+
+F32 = mybir.dt.float32
+BF16 = mybir.dt.bfloat16
+I32 = mybir.dt.int32
+U32 = mybir.dt.uint32
+U16 = mybir.dt.uint16
+U8 = mybir.dt.uint8
+FP8X4 = mybir.dt.float8_e4m3fn_x4
+FP4X4 = mybir.dt.float4_e2m1fn_x4
+ACT = mybir.ActivationFunctionType
+ALU = mybir.AluOpType
+
+P = 128
+PACK = 4
+KP = 512
+NPASS = 2
+JB = 128
+JH = 256
+GP_ADDS = 4
+
+
+def tile_list_acid_tie_strength_kernel(tc, tab_words, tab_scales, offs, offs2, w4_words, w4_scales, wg, prior, out):
+    nc = tc.nc
+    with ExitStack() as ctx:
+        keep = ctx.enter_context(tc.tile_pool(name="keep", bufs=1))
+        psum = ctx.enter_context(tc.psum_pool(name="psum", bufs=1))
+
+        def sb(name, shape, dtype):
+            return keep.tile(shape, dtype, name=name, align_bytes=64)
+
+        idx = keep.tile([P, S // 16], U16, name="idx")
+        idx2 = keep.tile([P, S2 // 16], U16, name="idx2")
+        tab = [sb(f"tab{a}", [P, T], U32) for a in range(NPASS)]
+        tsc_packed = sb("tsc_packed", [P, T], U8)
+        tsc_b = sb("tsc_b", [P, T], U8)
+        w4_raw = sb("w4_raw", [P, NPASS * K], U16)
+        w4s_raw = sb("w4s_raw", [P, NPASS * K], U8)
+        w4_dealt = sb("w4_dealt", [P, NPASS * K], U16)
+        w4s_dealt = sb("w4s_dealt", [P, NPASS * K], U8)
+
+        nc.vector.memset(w4s_raw[:].bitcast(I32), 0)
+        nc.vector.memset(tsc_packed[:].bitcast(I32), 0)
+        nc.vector.memset(tsc_b[:].bitcast(I32), 0)
+
+        def load_tab(a):
+            nc.sync.dma_start(out=tab[a][:].bitcast(I32), in_=tab_words[a].rearrange("p t i -> p (t i)").bitcast(I32))
+
+        wg_raw = {}
+
+        def load_wg(a, b):
+            raw = sb(f"wg_raw{a}{b}", [P, PACK, KP], F32)
+            nc.sync.dma_start(out=raw[:], in_=wg[KP * a : KP * (a + 1), KP * b : KP * (b + 1)].rearrange("(p i) c -> p i c", i=PACK))
+            wg_raw[a, b] = raw
+
+        def load_b(q):
+            nc.gpsimd.dma_start(out=tsc_b[32 * q : 32 * q + 4, :].bitcast(I32), in_=tab_scales[1, 4 * q : 4 * q + 4, :].bitcast(I32))
+
+        wg_order = [(1, 0), (1, 1), (0, 0), (0, 1)]
+
+        nc.sync.dma_start(
+            out=w4_raw[:].bitcast(I32).rearrange("p (a w) -> p a w", a=NPASS),
+            in_=w4_words.bitcast(I32).rearrange("a p w -> p a w"),
+        )
+        for q in range(4):
+            nc.sync.dma_start(
+                out=w4s_raw[32 * q : 32 * q + 4, :].bitcast(I32).rearrange("r (a w) -> r a w", a=NPASS),
+                in_=w4_scales[:, 4 * q : 4 * q + 4, :].bitcast(I32).rearrange("a r w -> r a w"),
+            )
+        nc.sync.dma_start(idx[:], offs)
+        load_tab(0)
+        nc.sync.dma_start(idx2[:], offs2)
+        for q in range(4):
+            nc.gpsimd.dma_start(out=tsc_packed[32 * q : 32 * q + 8, :].bitcast(I32), in_=tab_scales[:, 4 * q : 4 * q + 4, :].bitcast(I32))
+        for q in range(4):
+            load_b(q)
+        for ab in wg_order:
+            load_wg(*ab)
+        load_tab(1)
+        prior_sb = []
+        for h in range(2):
+            pr = sb(f"prior{h}", [P, S2 // P, JH], F32)
+            nc.sync.dma_start(out=pr[:], in_=prior[:, JH * h : JH * (h + 1)].rearrange("(mt p) j -> p mt j", p=P))
+            prior_sb.append(pr)
+
+        for a in range(NPASS):
+            cols = slice(K * a, K * (a + 1))
+            nc.vector.tensor_copy(
+                out=w4_dealt[:, cols].rearrange("p (b t m) -> p b t m", b=2, t=PACK),
+                in_=w4_raw[:, cols].rearrange("p (b m t) -> p b t m", b=2, t=PACK),
+            )
+
+        for a in range(NPASS):
+            cols = slice(K * a, K * (a + 1))
+            nc.vector.tensor_copy(
+                out=w4s_dealt[:, cols].rearrange("p (b t m) -> p b t m", b=2, t=PACK),
+                in_=w4s_raw[:, cols].rearrange("p (b m t) -> p b t m", b=2, t=PACK),
+            )
+
+        v_words = {}
+        v_scales = {}
+        v2_words = {}
+        v2_scales = {}
+
+        def gather(name, dtype, window, offsets, n):
+            g = sb(name, [P, n], dtype)
+            nc.vector.tensor_copy(g[:], window[:].indirect(offsets))
+            return g
+
+        v_words[0, 0] = gather("v0", U32, tab[0], idx[:], S)
+        v_scales[0] = gather("vs0", U8, tsc_packed, idx[:], S)
+        for g in range(2):
+            v2_words[0, g] = gather(f"v2_0{g}", U32, tab[0], idx2[:, 32 * g : 32 * (g + 1)], 512)
+        for g in range(2):
+            v2_scales[g] = gather(f"v2s{g}", U8, tsc_packed, idx2[:, 32 * g : 32 * (g + 1)], 512)
+
+        wg_codes = {}
+        wg_scales = {}
+        for n, (a, b) in enumerate(wg_order):
+            grouped = sb(f"wg_grouped{a}{b}", [P, PACK * KP], BF16)
+            dst = grouped[:].rearrange("p (t m i) -> p m t i", t=PACK, i=PACK)
+            src = wg_raw[a, b][:].rearrange("p i (m t) -> p m t i", t=PACK)
+            if n < 3:
+                nc.scalar.activation(out=dst, in_=src, func=ACT.Copy, scale=-1.0)
+            else:
+                nc.vector.tensor_scalar(out=dst, in0=src, scalar1=-1.0, scalar2=None, op0=ALU.mult)
+            codes = sb(f"wg_codes{a}{b}", [P, KP], U32)
+            scales = sb(f"wg_scales{a}{b}", [P, KP], U8)
+            nc.vector.quantize_mx(out=codes[:].bitcast(FP8X4), scales=scales[:], in_=grouped[:])
+            wg_codes[a, b] = codes
+            wg_scales[a, b] = scales
+
+        v_scales[1] = gather("vs1", U8, tsc_b, idx[:], S)
+
+        banks = {}
+        for jb in range(4):
+            for b in range(2):
+                banks[b, jb] = psum.tile([P, PACK, JB], F32, name=f"d{b}{jb}", tag=f"bank{2 * jb + b}")
+
+        def v_operand(a, jb):
+            if a == 0:
+                words = v_words[0, 0][:, JB * jb : JB * (jb + 1)]
+            else:
+                words = v_words[1, jb // 2][:, JB * (jb % 2) : JB * (jb % 2 + 1)]
+            return words.bitcast(FP8X4), v_scales[a][:, JB * jb : JB * (jb + 1)]
+
+        def w4_passes(a, b, jb, first):
+            rhs, rhs_scale = v_operand(a, jb)
+            for t in range(PACK):
+                c0 = K * a + KP * b + P * t
+                nc.tensor.matmul_mx(
+                    out=banks[b, jb][:, t, :], lhsT=w4_dealt[:, c0 : c0 + P].bitcast(FP4X4), lhsT_scale=w4s_dealt[:, c0 : c0 + P],
+                    rhs=rhs, rhs_scale=rhs_scale, start=(first and t == 0), stop=False,
+                )
+
+        def wg_passes(a, b, jb, last):
+            rhs, rhs_scale = v_operand(a, jb)
+            for t in range(PACK):
+                cols = slice(P * t, P * (t + 1))
+                nc.tensor.matmul_mx(
+                    out=banks[b, jb][:, t, :], lhsT=wg_codes[a, b][:, cols].bitcast(FP8X4), lhsT_scale=wg_scales[a, b][:, cols],
+                    rhs=rhs, rhs_scale=rhs_scale, start=False, stop=(last and t == PACK - 1),
+                )
+
+        for b in range(2):
+            for jb in range(4):
+                w4_passes(0, b, jb, True)
+        for b in range(2):
+            for jb in range(4):
+                wg_passes(0, b, jb, False)
+
+        for h in range(2):
+            v_words[1, h] = gather(f"v1{h}", U32, tab[1], idx[:, 16 * h : 16 * (h + 1)], JH)
+        for g in range(2):
+            v2_words[1, g] = gather(f"v2_1{g}", U32, tab[1], idx2[:, 32 * g : 32 * (g + 1)], 512)
+
+        h_codes = {}
+        h_scales = {}
+        for h in range(2):
+            for b in range(2):
+                grouped = sb(f"h_grouped{h}{b}", [P, JH * PACK], BF16)
+                for u in range(2):
+                    jb = 2 * h + u
+                    w4_passes(1, b, jb, False)
+                    wg_passes(1, b, jb, True)
+                    nc.scalar.activation(
+                        out=grouped[:, JB * PACK * u : JB * PACK * (u + 1)].rearrange("p (n t) -> p n t", t=PACK),
+                        in_=banks[b, jb][:].rearrange("p t n -> p n t"),
+                        func=ACT.Abs,
+                    )
+                codes = sb(f"h_codes{h}{b}", [P, JH], U32)
+                scales = sb(f"h_scales{h}{b}", [P, JH], U8)
+                nc.vector.quantize_mx(out=codes[:].bitcast(FP8X4), scales=scales[:], in_=grouped[:])
+                h_codes[h, b] = codes
+                h_scales[h, b] = scales
+
+        out_view = out.rearrange("(mt p) j -> p mt j", p=P)
+        for h in range(2):
+            for mp in range(4):
+                n = 4 * h + mp
+                e = psum.tile([P, 2, JH], F32, name=f"e{n}", tag=f"bank{n}")
+                for u in range(2):
+                    mt = 2 * mp + u
+                    cols = slice(P * (mt % 4), P * (mt % 4 + 1))
+                    for b in range(2):
+                        nc.tensor.matmul_mx(
+                            out=e[:, u, :], lhsT=v2_words[b, mt // 4][:, cols].bitcast(FP8X4), lhsT_scale=v2_scales[mt // 4][4 * b :, cols],
+                            rhs=h_codes[h, b][:].bitcast(FP8X4), rhs_scale=h_scales[h, b][:], start=(b == 0), stop=(b == 1),
+                        )
+                bounded = sb(f"bounded{n}", [P, 2, JH], F32)
+                weighted = sb(f"weighted{n}", [P, 2, JH], F32)
+                result = sb(f"result{n}", [P, 2, JH], F32)
+                nc.scalar.activation(out=bounded[:], in_=e[:], func=ACT.Tanh)
+                nc.vector.tensor_tensor(out=weighted[:], in0=e[:], in1=prior_sb[h][:, 2 * mp : 2 * mp + 2, :], op=ALU.mult)
+                adder = nc.gpsimd if n < GP_ADDS else nc.vector
+                adder.tensor_tensor(out=result[:], in0=bounded[:], in1=weighted[:], op=ALU.add)
+                nc.sync.dma_start(out=out_view[:, 2 * mp : 2 * mp + 2, JH * h : JH * (h + 1)], in_=result[:])

@@ -22,30 +22,38 @@ KP = 512
 NPASS = 2
 JB = 128
 JH = 256
-GP_ADDS = 4
+GP_ADDS = 5
 
 
 def tile_list_acid_tie_strength_kernel(tc, tab_words, tab_scales, offs, offs2, w4_words, w4_scales, wg, prior, out):
     nc = tc.nc
     with ExitStack() as ctx:
         keep = ctx.enter_context(tc.tile_pool(name="keep", bufs=1))
+        ring = ctx.enter_context(tc.tile_pool(name="ring", bufs=1))
         psum = ctx.enter_context(tc.psum_pool(name="psum", bufs=1))
 
-        def sb(name, shape, dtype):
-            return keep.tile(shape, dtype, name=name, align_bytes=64)
+        def sb(name, shape, dtype, at=None):
+            if at is None:
+                return keep.tile(shape, dtype, name=name, align_bytes=64)
+            return ring.tile(shape, dtype, name=name, align_bytes=64, offset=at)
+
+        raw_at = {(0, 0): 0, (1, 0): 10240, (0, 1): 26624, (1, 1): 0}
+        grouped_at = {(0, 0): 34816, (1, 0): 38912, (0, 1): 43008, (1, 1): 47104}
+
+        codes_at = {(0, 0): 51200, (1, 0): 53248}
 
         idx = keep.tile([P, S // 16], U16, name="idx")
         idx2 = keep.tile([P, S2 // 16], U16, name="idx2")
-        tab = [sb(f"tab{a}", [P, T], U32) for a in range(NPASS)]
-        tsc_packed = sb("tsc_packed", [P, T], U8)
-        tsc_b = sb("tsc_b", [P, T], U8)
-        w4_raw = sb("w4_raw", [P, NPASS * K], U16)
-        w4s_raw = sb("w4s_raw", [P, NPASS * K], U8)
+        tab = [sb("tab0", [P, T], U32), sb("tab1", [P, T], U32, 18432)]
+        tsc_packed = sb("tsc_packed", [P, T], U8, 51200)
+        tsc_b = sb("tsc_b", [P, T], U8, 53248)
+        w4_raw = sb("w4_raw", [P, NPASS * K], U16, 7168)
+        w4s_raw = sb("w4s_raw", [P, NPASS * K], U8, 25600)
         w4_dealt = sb("w4_dealt", [P, NPASS * K], U16)
         w4s_dealt = sb("w4s_dealt", [P, NPASS * K], U8)
 
         nc.vector.memset(w4s_raw[:].bitcast(I32), 0)
-        nc.vector.memset(tsc_packed[:].bitcast(I32), 0)
+        nc.gpsimd.memset(tsc_packed[:].bitcast(I32), 0)
         nc.vector.memset(tsc_b[:].bitcast(I32), 0)
 
         def load_tab(a):
@@ -54,88 +62,80 @@ def tile_list_acid_tie_strength_kernel(tc, tab_words, tab_scales, offs, offs2, w
         wg_raw = {}
 
         def load_wg(a, b):
-            raw = sb(f"wg_raw{a}{b}", [P, PACK, KP], F32)
+            raw = sb(f"wg_raw{a}{b}", [P, PACK, KP], F32, raw_at[a, b])
             nc.sync.dma_start(out=raw[:], in_=wg[KP * a : KP * (a + 1), KP * b : KP * (b + 1)].rearrange("(p i) c -> p i c", i=PACK))
             wg_raw[a, b] = raw
 
-        def load_b(q):
-            nc.gpsimd.dma_start(out=tsc_b[32 * q : 32 * q + 4, :].bitcast(I32), in_=tab_scales[1, 4 * q : 4 * q + 4, :].bitcast(I32))
+        prior_sb = []
 
-        wg_order = [(1, 0), (1, 1), (0, 0), (0, 1)]
+        def load_prior(h, at):
+            pr = sb(f"prior{h}", [P, S2 // P, JH], F32, at)
+            nc.sync.dma_start(out=pr[:], in_=prior[:, JH * h : JH * (h + 1)].rearrange("(mt p) j -> p mt j", p=P))
+            prior_sb.append(pr)
 
         nc.sync.dma_start(
             out=w4_raw[:].bitcast(I32).rearrange("p (a w) -> p a w", a=NPASS),
             in_=w4_words.bitcast(I32).rearrange("a p w -> p a w"),
         )
+        nc.sync.dma_start(idx[:], offs)
+        nc.sync.dma_start(idx2[:], offs2)
+        load_tab(0)
         for q in range(4):
-            nc.sync.dma_start(
+            nc.scalar.dma_start(
                 out=w4s_raw[32 * q : 32 * q + 4, :].bitcast(I32).rearrange("r (a w) -> r a w", a=NPASS),
                 in_=w4_scales[:, 4 * q : 4 * q + 4, :].bitcast(I32).rearrange("a r w -> r a w"),
             )
-        nc.sync.dma_start(idx[:], offs)
-        load_tab(0)
-        nc.sync.dma_start(idx2[:], offs2)
         for q in range(4):
-            nc.gpsimd.dma_start(out=tsc_packed[32 * q : 32 * q + 8, :].bitcast(I32), in_=tab_scales[:, 4 * q : 4 * q + 4, :].bitcast(I32))
+            queue = nc.gpsimd if q == 3 else nc.scalar
+            queue.dma_start(out=tsc_packed[32 * q : 32 * q + 8, :].bitcast(I32), in_=tab_scales[:, 4 * q : 4 * q + 4, :].bitcast(I32))
         for q in range(4):
-            load_b(q)
-        for ab in wg_order:
-            load_wg(*ab)
+            nc.scalar.dma_start(out=tsc_b[32 * q : 32 * q + 4, :].bitcast(I32), in_=tab_scales[1, 4 * q : 4 * q + 4, :].bitcast(I32))
+
+        def deal(dst, src):
+            for a in range(NPASS):
+                cols = slice(K * a, K * (a + 1))
+                nc.vector.tensor_copy(
+                    out=dst[:, cols].rearrange("p (b t m) -> p b t m", b=2, t=PACK),
+                    in_=src[:, cols].rearrange("p (b m t) -> p b t m", b=2, t=PACK),
+                )
+
+        deal(w4_dealt, w4_raw)
+        deal(w4s_dealt, w4s_raw)
+
+        load_wg(0, 0)
+        load_wg(1, 0)
         load_tab(1)
-        prior_sb = []
-        for h in range(2):
-            pr = sb(f"prior{h}", [P, S2 // P, JH], F32)
-            nc.sync.dma_start(out=pr[:], in_=prior[:, JH * h : JH * (h + 1)].rearrange("(mt p) j -> p mt j", p=P))
-            prior_sb.append(pr)
-
-        for a in range(NPASS):
-            cols = slice(K * a, K * (a + 1))
-            nc.vector.tensor_copy(
-                out=w4_dealt[:, cols].rearrange("p (b t m) -> p b t m", b=2, t=PACK),
-                in_=w4_raw[:, cols].rearrange("p (b m t) -> p b t m", b=2, t=PACK),
-            )
-
-        for a in range(NPASS):
-            cols = slice(K * a, K * (a + 1))
-            nc.vector.tensor_copy(
-                out=w4s_dealt[:, cols].rearrange("p (b t m) -> p b t m", b=2, t=PACK),
-                in_=w4s_raw[:, cols].rearrange("p (b m t) -> p b t m", b=2, t=PACK),
-            )
+        load_wg(0, 1)
 
         v_words = {}
         v_scales = {}
         v2_words = {}
         v2_scales = {}
 
-        def gather(name, dtype, window, offsets, n):
-            g = sb(name, [P, n], dtype)
-            nc.vector.tensor_copy(g[:], window[:].indirect(offsets))
-            return g
+        def gather(name, dtype, window, offsets, n, at=None):
+            picked = sb(name, [P, n], dtype, at)
+            nc.vector.tensor_copy(picked[:], window[:].indirect(offsets))
+            return picked
 
-        v_words[0, 0] = gather("v0", U32, tab[0], idx[:], S)
-        v_scales[0] = gather("vs0", U8, tsc_packed, idx[:], S)
-        for g in range(2):
-            v2_words[0, g] = gather(f"v2_0{g}", U32, tab[0], idx2[:, 32 * g : 32 * (g + 1)], 512)
-        for g in range(2):
-            v2_scales[g] = gather(f"v2s{g}", U8, tsc_packed, idx2[:, 32 * g : 32 * (g + 1)], 512)
+        def list2(g):
+            return idx2[:, 32 * g : 32 * (g + 1)]
 
         wg_codes = {}
         wg_scales = {}
-        for n, (a, b) in enumerate(wg_order):
-            grouped = sb(f"wg_grouped{a}{b}", [P, PACK * KP], BF16)
+
+        def quantise_wg(a, b, on_scalar):
+            grouped = sb(f"wg_grouped{a}{b}", [P, PACK * KP], BF16, grouped_at[a, b])
             dst = grouped[:].rearrange("p (t m i) -> p m t i", t=PACK, i=PACK)
             src = wg_raw[a, b][:].rearrange("p i (m t) -> p m t i", t=PACK)
-            if n < 3:
-                nc.scalar.activation(out=dst, in_=src, func=ACT.Copy, scale=-1.0)
-            else:
-                nc.vector.tensor_scalar(out=dst, in0=src, scalar1=-1.0, scalar2=None, op0=ALU.mult)
-            codes = sb(f"wg_codes{a}{b}", [P, KP], U32)
+            if on_scalar > 0:
+                nc.scalar.activation(out=dst[:, :on_scalar], in_=src[:, :on_scalar], func=ACT.Copy, scale=-1.0)
+            if on_scalar < P:
+                nc.vector.tensor_scalar(out=dst[:, on_scalar:], in0=src[:, on_scalar:], scalar1=-1.0, scalar2=None, op0=ALU.mult)
+            codes = sb(f"wg_codes{a}{b}", [P, KP], U32, codes_at.get((a, b)))
             scales = sb(f"wg_scales{a}{b}", [P, KP], U8)
             nc.vector.quantize_mx(out=codes[:].bitcast(FP8X4), scales=scales[:], in_=grouped[:])
             wg_codes[a, b] = codes
             wg_scales[a, b] = scales
-
-        v_scales[1] = gather("vs1", U8, tsc_b, idx[:], S)
 
         banks = {}
         for jb in range(4):
@@ -143,80 +143,94 @@ def tile_list_acid_tie_strength_kernel(tc, tab_words, tab_scales, offs, offs2, w
                 banks[b, jb] = psum.tile([P, PACK, JB], F32, name=f"d{b}{jb}", tag=f"bank{2 * jb + b}")
 
         def v_operand(a, jb):
-            if a == 0:
-                words = v_words[0, 0][:, JB * jb : JB * (jb + 1)]
-            else:
-                words = v_words[1, jb // 2][:, JB * (jb % 2) : JB * (jb % 2 + 1)]
+            words = v_words[a, jb // 2][:, JB * (jb % 2) : JB * (jb % 2 + 1)]
             return words.bitcast(FP8X4), v_scales[a][:, JB * jb : JB * (jb + 1)]
 
-        def w4_passes(a, b, jb, first):
-            rhs, rhs_scale = v_operand(a, jb)
-            for t in range(PACK):
-                c0 = K * a + KP * b + P * t
-                nc.tensor.matmul_mx(
-                    out=banks[b, jb][:, t, :], lhsT=w4_dealt[:, c0 : c0 + P].bitcast(FP4X4), lhsT_scale=w4s_dealt[:, c0 : c0 + P],
-                    rhs=rhs, rhs_scale=rhs_scale, start=(first and t == 0), stop=False,
-                )
-
-        def wg_passes(a, b, jb, last):
-            rhs, rhs_scale = v_operand(a, jb)
-            for t in range(PACK):
-                cols = slice(P * t, P * (t + 1))
-                nc.tensor.matmul_mx(
-                    out=banks[b, jb][:, t, :], lhsT=wg_codes[a, b][:, cols].bitcast(FP8X4), lhsT_scale=wg_scales[a, b][:, cols],
-                    rhs=rhs, rhs_scale=rhs_scale, start=False, stop=(last and t == PACK - 1),
-                )
-
-        for b in range(2):
+        def w4_passes(a, b):
             for jb in range(4):
-                w4_passes(0, b, jb, True)
-        for b in range(2):
-            for jb in range(4):
-                wg_passes(0, b, jb, False)
+                rhs, rhs_scale = v_operand(a, jb)
+                for t in range(PACK):
+                    c0 = K * a + KP * b + P * t
+                    nc.tensor.matmul_mx(
+                        out=banks[b, jb][:, t, :], lhsT=w4_dealt[:, c0 : c0 + P].bitcast(FP4X4), lhsT_scale=w4s_dealt[:, c0 : c0 + P],
+                        rhs=rhs, rhs_scale=rhs_scale, start=(a == 0 and t == 0), stop=False,
+                    )
 
-        for h in range(2):
-            v_words[1, h] = gather(f"v1{h}", U32, tab[1], idx[:, 16 * h : 16 * (h + 1)], JH)
+        def wg_passes(a, b):
+            for jb in range(4):
+                rhs, rhs_scale = v_operand(a, jb)
+                for t in range(PACK):
+                    cols = slice(P * t, P * (t + 1))
+                    nc.tensor.matmul_mx(
+                        out=banks[b, jb][:, t, :], lhsT=wg_codes[a, b][:, cols].bitcast(FP8X4), lhsT_scale=wg_scales[a, b][:, cols],
+                        rhs=rhs, rhs_scale=rhs_scale, start=False, stop=(a == 1 and t == PACK - 1),
+                    )
+
+        v0 = gather("v0", U32, tab[0], idx[:], S)
+        v_words[0, 0] = v0[:, :JH]
+        v_words[0, 1] = v0[:, JH:]
+        v_scales[0] = gather("vs0", U8, tsc_packed, idx[:], S)
+        v2_words[0, 0] = gather("v2_00", U32, tab[0], list2(0), 512)
         for g in range(2):
-            v2_words[1, g] = gather(f"v2_1{g}", U32, tab[1], idx2[:, 32 * g : 32 * (g + 1)], 512)
+            v2_scales[g] = gather(f"v2s{g}", U8, tsc_packed, list2(g), 512)
+        for b in range(2):
+            w4_passes(0, b)
+
+        quantise_wg(0, 0, P)
+        load_wg(1, 1)
+        wg_passes(0, 0)
+
+        v_scales[1] = gather("vs1", U8, tsc_b, idx[:], S, grouped_at[0, 0])
+        v1 = gather("v1", U32, tab[1], idx[:], S)
+        v_words[1, 0] = v1[:, :JH]
+        v_words[1, 1] = v1[:, JH:]
+        w4_passes(1, 0)
+
+        quantise_wg(1, 0, P)
+        load_prior(0, raw_at[1, 0])
+        wg_passes(1, 0)
+        w4_passes(1, 1)
+
+        v2_words[1, 0] = gather("v2_10", U32, tab[1], list2(0), 512)
+
+        quantise_wg(0, 1, P)
+        load_prior(1, raw_at[0, 1])
+        wg_passes(0, 1)
+        quantise_wg(1, 1, 0)
+        wg_passes(1, 1)
+        for a in range(NPASS):
+            v2_words[a, 1] = gather(f"v2_{a}1", U32, tab[a], list2(1), 512, grouped_at[1, 1] + 2048 * a)
 
         h_codes = {}
         h_scales = {}
-        for h in range(2):
+        for jb in range(4):
+            grouped = sb(f"h_grouped{jb}", [P, 2, JB, PACK], BF16)
             for b in range(2):
-                grouped = sb(f"h_grouped{h}{b}", [P, JH * PACK], BF16)
-                for u in range(2):
-                    jb = 2 * h + u
-                    w4_passes(1, b, jb, False)
-                    wg_passes(1, b, jb, True)
-                    nc.scalar.activation(
-                        out=grouped[:, JB * PACK * u : JB * PACK * (u + 1)].rearrange("p (n t) -> p n t", t=PACK),
-                        in_=banks[b, jb][:].rearrange("p t n -> p n t"),
-                        func=ACT.Abs,
-                    )
-                codes = sb(f"h_codes{h}{b}", [P, JH], U32)
-                scales = sb(f"h_scales{h}{b}", [P, JH], U8)
-                nc.vector.quantize_mx(out=codes[:].bitcast(FP8X4), scales=scales[:], in_=grouped[:])
-                h_codes[h, b] = codes
-                h_scales[h, b] = scales
+                nc.scalar.activation(out=grouped[:, b, :, :], in_=banks[b, jb][:].rearrange("p t n -> p n t"), func=ACT.Abs)
+            codes = sb(f"h_codes{jb}", [P, 2 * JB], U32)
+            scales = sb(f"h_scales{jb}", [P, 2 * JB], U8)
+            nc.vector.quantize_mx(out=codes[:].bitcast(FP8X4), scales=scales[:], in_=grouped[:].rearrange("p b n t -> p (b n t)"))
+            h_codes[jb] = codes
+            h_scales[jb] = scales
 
         out_view = out.rearrange("(mt p) j -> p mt j", p=P)
-        for h in range(2):
-            for mp in range(4):
-                n = 4 * h + mp
-                e = psum.tile([P, 2, JH], F32, name=f"e{n}", tag=f"bank{n}")
-                for u in range(2):
-                    mt = 2 * mp + u
-                    cols = slice(P * (mt % 4), P * (mt % 4 + 1))
+        for jb in range(4):
+            for g in range(2):
+                n = 2 * jb + g
+                e = psum.tile([P, 4, JB], F32, name=f"e{n}", tag=f"bank{n}")
+                for u in range(4):
+                    cols = slice(P * u, P * (u + 1))
                     for b in range(2):
+                        hc = slice(JB * b, JB * (b + 1))
                         nc.tensor.matmul_mx(
-                            out=e[:, u, :], lhsT=v2_words[b, mt // 4][:, cols].bitcast(FP8X4), lhsT_scale=v2_scales[mt // 4][4 * b :, cols],
-                            rhs=h_codes[h, b][:].bitcast(FP8X4), rhs_scale=h_scales[h, b][:], start=(b == 0), stop=(b == 1),
+                            out=e[:, u, :], lhsT=v2_words[b, g][:, cols].bitcast(FP8X4), lhsT_scale=v2_scales[g][4 * b :, cols],
+                            rhs=h_codes[jb][:, hc].bitcast(FP8X4), rhs_scale=h_scales[jb][:, hc], start=(b == 0), stop=(b == 1),
                         )
-                bounded = sb(f"bounded{n}", [P, 2, JH], F32)
-                weighted = sb(f"weighted{n}", [P, 2, JH], F32)
-                result = sb(f"result{n}", [P, 2, JH], F32)
+                bounded = sb(f"bounded{n}", [P, 4, JB], F32)
+                weighted = sb(f"weighted{n}", [P, 4, JB], F32)
+                result = sb(f"result{n}", [P, 4, JB], F32)
                 nc.scalar.activation(out=bounded[:], in_=e[:], func=ACT.Tanh)
-                nc.vector.tensor_tensor(out=weighted[:], in0=e[:], in1=prior_sb[h][:, 2 * mp : 2 * mp + 2, :], op=ALU.mult)
+                nc.vector.tensor_tensor(out=weighted[:], in0=e[:], in1=prior_sb[jb // 2][:, 4 * g : 4 * g + 4, JB * (jb % 2) : JB * (jb % 2 + 1)], op=ALU.mult)
                 adder = nc.gpsimd if n < GP_ADDS else nc.vector
                 adder.tensor_tensor(out=result[:], in0=bounded[:], in1=weighted[:], op=ALU.add)
-                nc.sync.dma_start(out=out_view[:, 2 * mp : 2 * mp + 2, JH * h : JH * (h + 1)], in_=result[:])
+                nc.sync.dma_start(out=out_view[:, 4 * g : 4 * g + 4, JB * jb : JB * (jb + 1)], in_=result[:])

@@ -22,7 +22,7 @@ KP = 512
 NPASS = 2
 JB = 128
 JH = 256
-GP_ADDS = 5
+GP_ADDS = 4
 
 
 def tile_list_acid_tie_strength_kernel(tc, tab_words, tab_scales, offs, offs2, w4_words, w4_scales, wg, prior, out):
@@ -123,14 +123,16 @@ def tile_list_acid_tie_strength_kernel(tc, tab_words, tab_scales, offs, offs2, w
         wg_codes = {}
         wg_scales = {}
 
-        def quantise_wg(a, b, on_scalar):
+        def quantise_wg(a, b, halves=None):
             grouped = sb(f"wg_grouped{a}{b}", [P, PACK * KP], BF16, grouped_at[a, b])
-            dst = grouped[:].rearrange("p (t m i) -> p m t i", t=PACK, i=PACK)
-            src = wg_raw[a, b][:].rearrange("p i (m t) -> p m t i", t=PACK)
-            if on_scalar > 0:
-                nc.scalar.activation(out=dst[:, :on_scalar], in_=src[:, :on_scalar], func=ACT.Copy, scale=-1.0)
-            if on_scalar < P:
-                nc.vector.tensor_scalar(out=dst[:, on_scalar:], in0=src[:, on_scalar:], scalar1=-1.0, scalar2=None, op0=ALU.mult)
+            dst = grouped[:].rearrange("p (t m i) -> p m i t", t=PACK, i=PACK)
+            if halves is None:
+                src = wg_raw[a, b][:].rearrange("p i (m t) -> p m i t", t=PACK)
+                nc.scalar.activation(out=dst, in_=src, func=ACT.Copy, scale=-1.0)
+            else:
+                for u in range(2):
+                    src = halves[u][:].rearrange("p i (m t) -> p m i t", t=PACK)
+                    nc.vector.tensor_scalar(out=dst[:, 64 * u : 64 * (u + 1)], in0=src, scalar1=-1.0, scalar2=None, op0=ALU.mult)
             codes = sb(f"wg_codes{a}{b}", [P, KP], U32, codes_at.get((a, b)))
             scales = sb(f"wg_scales{a}{b}", [P, KP], U8)
             nc.vector.quantize_mx(out=codes[:].bitcast(FP8X4), scales=scales[:], in_=grouped[:])
@@ -170,67 +172,84 @@ def tile_list_acid_tie_strength_kernel(tc, tab_words, tab_scales, offs, offs2, w
         v_words[0, 0] = v0[:, :JH]
         v_words[0, 1] = v0[:, JH:]
         v_scales[0] = gather("vs0", U8, tsc_packed, idx[:], S)
-        v2_words[0, 0] = gather("v2_00", U32, tab[0], list2(0), 512)
         for g in range(2):
             v2_scales[g] = gather(f"v2s{g}", U8, tsc_packed, list2(g), 512)
         for b in range(2):
             w4_passes(0, b)
 
-        quantise_wg(0, 0, P)
-        load_wg(1, 1)
+        quantise_wg(0, 0)
+        last_halves = []
+        for u in range(2):
+            raw = sb(f"wg_last{u}", [P, PACK, KP // 2], F32, raw_at[1, 1] + 4096 * u)
+            nc.sync.dma_start(out=raw[:], in_=wg[KP:, KP + JH * u : KP + JH * (u + 1)].rearrange("(p i) c -> p i c", i=PACK))
+            last_halves.append(raw)
         wg_passes(0, 0)
 
         v_scales[1] = gather("vs1", U8, tsc_b, idx[:], S, grouped_at[0, 0])
+        v2_words[0, 0] = gather("v2_00", U32, tab[0], list2(0), 512, grouped_at[0, 0] + 1024)
         v1 = gather("v1", U32, tab[1], idx[:], S)
         v_words[1, 0] = v1[:, :JH]
         v_words[1, 1] = v1[:, JH:]
         w4_passes(1, 0)
 
-        quantise_wg(1, 0, P)
+        quantise_wg(1, 0)
         load_prior(0, raw_at[1, 0])
         wg_passes(1, 0)
         w4_passes(1, 1)
 
         v2_words[1, 0] = gather("v2_10", U32, tab[1], list2(0), 512)
+        v2_words[0, 1] = gather("v2_01", U32, tab[0], list2(1), 512, grouped_at[1, 0])
 
-        quantise_wg(0, 1, P)
+        quantise_wg(0, 1)
         load_prior(1, raw_at[0, 1])
         wg_passes(0, 1)
-        quantise_wg(1, 1, 0)
+        quantise_wg(1, 1, last_halves)
         wg_passes(1, 1)
-        for a in range(NPASS):
-            v2_words[a, 1] = gather(f"v2_{a}1", U32, tab[a], list2(1), 512, grouped_at[1, 1] + 2048 * a)
+        v2_words[1, 1] = gather("v2_11", U32, tab[1], list2(1), 512, grouped_at[1, 1])
 
-        h_codes = {}
-        h_scales = {}
-        for jb in range(4):
-            grouped = sb(f"h_grouped{jb}", [P, 2, JB, PACK], BF16)
-            for b in range(2):
-                nc.scalar.activation(out=grouped[:, b, :, :], in_=banks[b, jb][:].rearrange("p t n -> p n t"), func=ACT.Abs)
-            codes = sb(f"h_codes{jb}", [P, 2 * JB], U32)
-            scales = sb(f"h_scales{jb}", [P, 2 * JB], U8)
-            nc.vector.quantize_mx(out=codes[:].bitcast(FP8X4), scales=scales[:], in_=grouped[:].rearrange("p b n t -> p (b n t)"))
-            h_codes[jb] = codes
-            h_scales[jb] = scales
+        h_codes = []
+        h_scales = []
+        for b in range(2):
+            grouped = sb(f"h_grouped{b}", [P, S, PACK], BF16)
+            codes = sb(f"h_codes{b}", [P, S], U32)
+            scales = sb(f"h_scales{b}", [P, S], U8)
+            done = 0
+            for jb in range(4):
+                nc.scalar.activation(out=grouped[:, JB * jb : JB * (jb + 1), :], in_=banks[b, jb][:].rearrange("p t n -> p n t"), func=ACT.Abs)
+                if jb == 3 or (b == 1 and jb < 2):
+                    cols = slice(done, JB * (jb + 1))
+                    nc.vector.quantize_mx(out=codes[:, cols].bitcast(FP8X4), scales=scales[:, cols], in_=grouped[:, cols, :].rearrange("p n t -> p (n t)"))
+                    done = JB * (jb + 1)
+            h_codes.append(codes)
+            h_scales.append(scales)
 
         out_view = out.rearrange("(mt p) j -> p mt j", p=P)
-        for jb in range(4):
-            for g in range(2):
-                n = 2 * jb + g
-                e = psum.tile([P, 4, JB], F32, name=f"e{n}", tag=f"bank{n}")
-                for u in range(4):
-                    cols = slice(P * u, P * (u + 1))
-                    for b in range(2):
-                        hc = slice(JB * b, JB * (b + 1))
-                        nc.tensor.matmul_mx(
-                            out=e[:, u, :], lhsT=v2_words[b, g][:, cols].bitcast(FP8X4), lhsT_scale=v2_scales[g][4 * b :, cols],
-                            rhs=h_codes[jb][:, hc].bitcast(FP8X4), rhs_scale=h_scales[jb][:, hc], start=(b == 0), stop=(b == 1),
-                        )
-                bounded = sb(f"bounded{n}", [P, 4, JB], F32)
-                weighted = sb(f"weighted{n}", [P, 4, JB], F32)
-                result = sb(f"result{n}", [P, 4, JB], F32)
-                nc.scalar.activation(out=bounded[:], in_=e[:], func=ACT.Tanh)
-                nc.vector.tensor_tensor(out=weighted[:], in0=e[:], in1=prior_sb[jb // 2][:, 4 * g : 4 * g + 4, JB * (jb % 2) : JB * (jb % 2 + 1)], op=ALU.mult)
-                adder = nc.gpsimd if n < GP_ADDS else nc.vector
-                adder.tensor_tensor(out=result[:], in0=bounded[:], in1=weighted[:], op=ALU.add)
-                nc.sync.dma_start(out=out_view[:, 4 * g : 4 * g + 4, JB * jb : JB * (jb + 1)], in_=result[:])
+
+        def match(n, bank, mt0, tiles, j0, width, result):
+            e = psum.tile([P, tiles, width], F32, name=f"e{n}", tag=f"bank{bank}")
+            jc = slice(j0, j0 + width)
+            for u in range(tiles):
+                g, r = divmod(mt0 + u, 4)
+                cols = slice(P * r, P * (r + 1))
+                for b in range(2):
+                    nc.tensor.matmul_mx(
+                        out=e[:, u, :], lhsT=v2_words[b, g][:, cols].bitcast(FP8X4), lhsT_scale=v2_scales[g][4 * b :, cols],
+                        rhs=h_codes[b][:, jc].bitcast(FP8X4), rhs_scale=h_scales[b][:, jc], start=(b == 0), stop=(b == 1),
+                    )
+            bounded = sb(f"bounded{n}", [P, tiles, width], F32)
+            weighted = sb(f"weighted{n}", [P, tiles, width], F32)
+            nc.vector.tensor_tensor(out=weighted[:], in0=e[:], in1=prior_sb[j0 // JH][:, mt0 : mt0 + tiles, j0 % JH : j0 % JH + width], op=ALU.mult)
+            nc.scalar.activation(out=bounded[:], in_=e[:], func=ACT.Tanh)
+            adder = nc.gpsimd if n < GP_ADDS else nc.vector
+            adder.tensor_tensor(out=result, in0=bounded[:], in1=weighted[:], op=ALU.add)
+
+        for g in range(2):
+            result = sb(f"result_first{g}", [P, 4, JH], F32)
+            for jb in range(2):
+                n = 2 * g + jb
+                match(n, 2 * n, 4 * g, 4, JB * jb, JB, result[:, :, JB * jb : JB * (jb + 1)])
+            nc.sync.dma_start(out=out_view[:, 4 * g : 4 * g + 4, :JH], in_=result[:])
+        for mp in range(4):
+            result = sb(f"result_second{mp}", [P, 2, JH], F32)
+            match(4 + mp, 2 * mp + 1, 2 * mp, 2, JH, JH, result[:])
+            nc.sync.dma_start(out=out_view[:, 2 * mp : 2 * mp + 2, JH:], in_=result[:])

@@ -44,11 +44,11 @@ def tile_list_acid_tie_strength_kernel(tc, tab_words, tab_scales, offs, offs2, w
 
         idx = keep.tile([P, S // 16], U16, name="idx")
         idx2 = keep.tile([P, S2 // 16], U16, name="idx2")
-        tab = [sb("tab0", [P, T], U32), sb("tab1", [P, T], U32, 18432)]
+        tab = [sb("tab0", [P, T], U32), sb("tab1", [P, T], U32)]
         tsc_packed = sb("tsc_packed", [P, T], U8, 51200)
         tsc_b = sb("tsc_b", [P, T], U8, 53248)
-        w4_raw = sb("w4_raw", [P, NPASS * K], U16, 7168)
-        w4s_raw = sb("w4s_raw", [P, NPASS * K], U8, 25600)
+        w4_raw = sb("w4_raw", [P, NPASS * K], U16)
+        w4s_raw = sb("w4s_raw", [P, NPASS * K], U8, raw_at[0, 1])
         w4_dealt = sb("w4_dealt", [P, NPASS * K], U16)
         w4s_dealt = sb("w4s_dealt", [P, NPASS * K], U8)
 
@@ -80,16 +80,17 @@ def tile_list_acid_tie_strength_kernel(tc, tab_words, tab_scales, offs, offs2, w
         nc.sync.dma_start(idx[:], offs)
         nc.sync.dma_start(idx2[:], offs2)
         load_tab(0)
+        load_wg(0, 0)
+        load_wg(1, 0)
+        load_tab(1)
+        w4s_rows = w4_scales.bitcast(I32).rearrange("a (q r) w -> r q a w", r=4)
+        for r in range(4):
+            nc.scalar.dma_start(out=w4s_raw[:].bitcast(I32)[r:P:32, :].rearrange("q (a w) -> q a w", a=NPASS), in_=w4s_rows[r])
         for q in range(4):
-            nc.scalar.dma_start(
-                out=w4s_raw[32 * q : 32 * q + 4, :].bitcast(I32).rearrange("r (a w) -> r a w", a=NPASS),
-                in_=w4_scales[:, 4 * q : 4 * q + 4, :].bitcast(I32).rearrange("a r w -> r a w"),
-            )
-        for q in range(4):
-            queue = nc.gpsimd if q == 3 else nc.scalar
-            queue.dma_start(out=tsc_packed[32 * q : 32 * q + 8, :].bitcast(I32), in_=tab_scales[:, 4 * q : 4 * q + 4, :].bitcast(I32))
-        for q in range(4):
-            nc.scalar.dma_start(out=tsc_b[32 * q : 32 * q + 4, :].bitcast(I32), in_=tab_scales[1, 4 * q : 4 * q + 4, :].bitcast(I32))
+            nc.gpsimd.dma_start(out=tsc_packed[32 * q : 32 * q + 8, :].bitcast(I32), in_=tab_scales[:, 4 * q : 4 * q + 4, :].bitcast(I32))
+        tsc_rows = tab_scales[1].bitcast(I32).rearrange("(q r) w -> r q w", r=4)
+        for r in range(4):
+            nc.gpsimd.dma_start(out=tsc_b[:].bitcast(I32)[r:P:32, :], in_=tsc_rows[r])
 
         def deal(dst, src):
             for a in range(NPASS):
@@ -102,9 +103,6 @@ def tile_list_acid_tie_strength_kernel(tc, tab_words, tab_scales, offs, offs2, w
         deal(w4_dealt, w4_raw)
         deal(w4s_dealt, w4s_raw)
 
-        load_wg(0, 0)
-        load_wg(1, 0)
-        load_tab(1)
         load_wg(0, 1)
 
         v_words = {}
@@ -186,8 +184,7 @@ def tile_list_acid_tie_strength_kernel(tc, tab_words, tab_scales, offs, offs2, w
         wg_passes(0, 0)
 
         v_scales[1] = gather("vs1", U8, tsc_b, idx[:], S, grouped_at[0, 0])
-        v2_words[0, 0] = gather("v2_00", U32, tab[0], list2(0), 512, grouped_at[0, 0] + 1024)
-        v1 = gather("v1", U32, tab[1], idx[:], S)
+        v1 = gather("v1", U32, tab[1], idx[:], S, grouped_at[0, 0] + 1024)
         v_words[1, 0] = v1[:, :JH]
         v_words[1, 1] = v1[:, JH:]
         w4_passes(1, 0)
@@ -197,15 +194,16 @@ def tile_list_acid_tie_strength_kernel(tc, tab_words, tab_scales, offs, offs2, w
         wg_passes(1, 0)
         w4_passes(1, 1)
 
-        v2_words[1, 0] = gather("v2_10", U32, tab[1], list2(0), 512)
-        v2_words[0, 1] = gather("v2_01", U32, tab[0], list2(1), 512, grouped_at[1, 0])
+        for a in range(NPASS):
+            v2_words[a, 0] = gather(f"v2_{a}0", U32, tab[a], list2(0), 512, grouped_at[1, 0] + 2048 * a)
 
         quantise_wg(0, 1)
         load_prior(1, raw_at[0, 1])
         wg_passes(0, 1)
         quantise_wg(1, 1, last_halves)
         wg_passes(1, 1)
-        v2_words[1, 1] = gather("v2_11", U32, tab[1], list2(1), 512, grouped_at[1, 1])
+        for a in range(NPASS):
+            v2_words[a, 1] = gather(f"v2_{a}1", U32, tab[a], list2(1), 512, grouped_at[1, 1] + 2048 * a)
 
         h_codes = []
         h_scales = []

from contextlib import ExitStack

import concourse.mybir as mybir

K, T, S, S2 = 1024, 2048, 512, 1024
FLOPS = 2 * K * K * S * 2 + 2 * K * S * S2

F32 = mybir.dt.float32
BF16 = mybir.dt.bfloat16
I32 = mybir.dt.int32
U32 = mybir.dt.uint32
U16 = mybir.dt.uint16
U8 = mybir.dt.uint8
FP8X4 = mybir.dt.float8_e4m3fn_x4
FP4X4 = mybir.dt.float4_e2m1fn_x4
ACT = mybir.ActivationFunctionType
ALU = mybir.AluOpType

P = 128
PACK = 4
KP = 512
NPASS = 2
JB = 128
JH = 256
GP_ADDS = 4


def tile_list_acid_tie_strength_kernel(tc, tab_words, tab_scales, offs, offs2, w4_words, w4_scales, wg, prior, out):
    nc = tc.nc
    with ExitStack() as ctx:
        keep = ctx.enter_context(tc.tile_pool(name="keep", bufs=1))
        ring = ctx.enter_context(tc.tile_pool(name="ring", bufs=1))
        psum = ctx.enter_context(tc.psum_pool(name="psum", bufs=1))

        def sb(name, shape, dtype, at=None):
            if at is None:
                return keep.tile(shape, dtype, name=name, align_bytes=64)
            return ring.tile(shape, dtype, name=name, align_bytes=64, offset=at)

        raw_at = {(0, 0): 0, (1, 0): 10240, (0, 1): 26624, (1, 1): 0}
        grouped_at = {(0, 0): 34816, (1, 0): 38912, (0, 1): 43008, (1, 1): 47104}

        codes_at = {(0, 0): 51200, (1, 0): 53248}

        idx = keep.tile([P, S // 16], U16, name="idx")
        idx2 = keep.tile([P, S2 // 16], U16, name="idx2")
        tab = [sb("tab0", [P, T], U32), sb("tab1", [P, T], U32)]
        tsc_packed = sb("tsc_packed", [P, T], U8, 51200)
        tsc_b = sb("tsc_b", [P, T], U8, 53248)
        w4_raw = sb("w4_raw", [P, NPASS * K], U16)
        w4s_raw = sb("w4s_raw", [P, NPASS * K], U8, raw_at[0, 1])
        w4_dealt = sb("w4_dealt", [P, NPASS * K], U16)
        w4s_dealt = sb("w4s_dealt", [P, NPASS * K], U8)

        nc.vector.memset(w4s_raw[:].bitcast(I32), 0)
        nc.gpsimd.memset(tsc_packed[:].bitcast(I32), 0)
        nc.vector.memset(tsc_b[:].bitcast(I32), 0)

        def load_tab(a):
            nc.sync.dma_start(out=tab[a][:].bitcast(I32), in_=tab_words[a].rearrange("p t i -> p (t i)").bitcast(I32))

        wg_raw = {}

        def load_wg(a, b):
            raw = sb(f"wg_raw{a}{b}", [P, PACK, KP], F32, raw_at[a, b])
            nc.sync.dma_start(out=raw[:], in_=wg[KP * a : KP * (a + 1), KP * b : KP * (b + 1)].rearrange("(p i) c -> p i c", i=PACK))
            wg_raw[a, b] = raw

        prior_sb = []

        def load_prior(h, at):
            pr = sb(f"prior{h}", [P, S2 // P, JH], F32, at)
            nc.sync.dma_start(out=pr[:], in_=prior[:, JH * h : JH * (h + 1)].rearrange("(mt p) j -> p mt j", p=P))
            prior_sb.append(pr)

        nc.sync.dma_start(
            out=w4_raw[:].bitcast(I32).rearrange("p (a w) -> p a w", a=NPASS),
            in_=w4_words.bitcast(I32).rearrange("a p w -> p a w"),
        )
        nc.sync.dma_start(idx[:], offs)
        nc.sync.dma_start(idx2[:], offs2)
        load_tab(0)
        load_wg(0, 0)
        load_wg(1, 0)
        load_tab(1)
        w4s_rows = w4_scales.bitcast(I32).rearrange("a (q r) w -> r q a w", r=4)
        for r in range(4):
            nc.scalar.dma_start(out=w4s_raw[:].bitcast(I32)[r:P:32, :].rearrange("q (a w) -> q a w", a=NPASS), in_=w4s_rows[r])
        for q in range(4):
            nc.gpsimd.dma_start(out=tsc_packed[32 * q : 32 * q + 8, :].bitcast(I32), in_=tab_scales[:, 4 * q : 4 * q + 4, :].bitcast(I32))
        tsc_rows = tab_scales[1].bitcast(I32).rearrange("(q r) w -> r q w", r=4)
        for r in range(4):
            nc.gpsimd.dma_start(out=tsc_b[:].bitcast(I32)[r:P:32, :], in_=tsc_rows[r])

        def deal(dst, src):
            for a in range(NPASS):
                cols = slice(K * a, K * (a + 1))
                nc.vector.tensor_copy(
                    out=dst[:, cols].rearrange("p (b t m) -> p b t m", b=2, t=PACK),
                    in_=src[:, cols].rearrange("p (b m t) -> p b t m", b=2, t=PACK),
                )

        deal(w4_dealt, w4_raw)
        deal(w4s_dealt, w4s_raw)

        load_wg(0, 1)

        v_words = {}
        v_scales = {}
        v2_words = {}
        v2_scales = {}

        def gather(name, dtype, window, offsets, n, at=None):
            picked = sb(name, [P, n], dtype, at)
            nc.vector.tensor_copy(picked[:], window[:].indirect(offsets))
            return picked

        def list2(g):
            return idx2[:, 32 * g : 32 * (g + 1)]

        wg_codes = {}
        wg_scales = {}

        def quantise_wg(a, b, halves=None):
            grouped = sb(f"wg_grouped{a}{b}", [P, PACK * KP], BF16, grouped_at[a, b])
            dst = grouped[:].rearrange("p (t m i) -> p m i t", t=PACK, i=PACK)
            if halves is None:
                src = wg_raw[a, b][:].rearrange("p i (m t) -> p m i t", t=PACK)
                nc.scalar.activation(out=dst, in_=src, func=ACT.Copy, scale=-1.0)
            else:
                for u in range(2):
                    src = halves[u][:].rearrange("p i (m t) -> p m i t", t=PACK)
                    nc.vector.tensor_scalar(out=dst[:, 64 * u : 64 * (u + 1)], in0=src, scalar1=-1.0, scalar2=None, op0=ALU.mult)
            codes = sb(f"wg_codes{a}{b}", [P, KP], U32, codes_at.get((a, b)))
            scales = sb(f"wg_scales{a}{b}", [P, KP], U8)
            nc.vector.quantize_mx(out=codes[:].bitcast(FP8X4), scales=scales[:], in_=grouped[:])
            wg_codes[a, b] = codes
            wg_scales[a, b] = scales

        banks = {}
        for jb in range(4):
            for b in range(2):
                banks[b, jb] = psum.tile([P, PACK, JB], F32, name=f"d{b}{jb}", tag=f"bank{2 * jb + b}")

        def v_operand(a, jb):
            words = v_words[a, jb // 2][:, JB * (jb % 2) : JB * (jb % 2 + 1)]
            return words.bitcast(FP8X4), v_scales[a][:, JB * jb : JB * (jb + 1)]

        def w4_passes(a, b):
            for jb in range(4):
                rhs, rhs_scale = v_operand(a, jb)
                for t in range(PACK):
                    c0 = K * a + KP * b + P * t
                    nc.tensor.matmul_mx(
                        out=banks[b, jb][:, t, :], lhsT=w4_dealt[:, c0 : c0 + P].bitcast(FP4X4), lhsT_scale=w4s_dealt[:, c0 : c0 + P],
                        rhs=rhs, rhs_scale=rhs_scale, start=(a == 0 and t == 0), stop=False,
                    )

        def wg_passes(a, b):
            for jb in range(4):
                rhs, rhs_scale = v_operand(a, jb)
                for t in range(PACK):
                    cols = slice(P * t, P * (t + 1))
                    nc.tensor.matmul_mx(
                        out=banks[b, jb][:, t, :], lhsT=wg_codes[a, b][:, cols].bitcast(FP8X4), lhsT_scale=wg_scales[a, b][:, cols],
                        rhs=rhs, rhs_scale=rhs_scale, start=False, stop=(a == 1 and t == PACK - 1),
                    )

        v0 = gather("v0", U32, tab[0], idx[:], S)
        v_words[0, 0] = v0[:, :JH]
        v_words[0, 1] = v0[:, JH:]
        v_scales[0] = gather("vs0", U8, tsc_packed, idx[:], S)
        for g in range(2):
            v2_scales[g] = gather(f"v2s{g}", U8, tsc_packed, list2(g), 512)
        for b in range(2):
            w4_passes(0, b)

        quantise_wg(0, 0)
        last_halves = []
        for u in range(2):
            raw = sb(f"wg_last{u}", [P, PACK, KP // 2], F32, raw_at[1, 1] + 4096 * u)
            nc.sync.dma_start(out=raw[:], in_=wg[KP:, KP + JH * u : KP + JH * (u + 1)].rearrange("(p i) c -> p i c", i=PACK))
            last_halves.append(raw)
        wg_passes(0, 0)

        v_scales[1] = gather("vs1", U8, tsc_b, idx[:], S, grouped_at[0, 0])
        v1 = gather("v1", U32, tab[1], idx[:], S, grouped_at[0, 0] + 1024)
        v_words[1, 0] = v1[:, :JH]
        v_words[1, 1] = v1[:, JH:]
        w4_passes(1, 0)

        quantise_wg(1, 0)
        load_prior(0, raw_at[1, 0])
        wg_passes(1, 0)
        w4_passes(1, 1)

        for a in range(NPASS):
            v2_words[a, 0] = gather(f"v2_{a}0", U32, tab[a], list2(0), 512, grouped_at[1, 0] + 2048 * a)

        quantise_wg(0, 1)
        load_prior(1, raw_at[0, 1])
        wg_passes(0, 1)
        quantise_wg(1, 1, last_halves)
        wg_passes(1, 1)
        for a in range(NPASS):
            v2_words[a, 1] = gather(f"v2_{a}1", U32, tab[a], list2(1), 512, grouped_at[1, 1] + 2048 * a)

        h_codes = []
        h_scales = []
        for b in range(2):
            grouped = sb(f"h_grouped{b}", [P, S, PACK], BF16)
            codes = sb(f"h_codes{b}", [P, S], U32)
            scales = sb(f"h_scales{b}", [P, S], U8)
            done = 0
            for jb in range(4):
                nc.scalar.activation(out=grouped[:, JB * jb : JB * (jb + 1), :], in_=banks[b, jb][:].rearrange("p t n -> p n t"), func=ACT.Abs)
                if jb == 3 or (b == 1 and jb < 2):
                    cols = slice(done, JB * (jb + 1))
                    nc.vector.quantize_mx(out=codes[:, cols].bitcast(FP8X4), scales=scales[:, cols], in_=grouped[:, cols, :].rearrange("p n t -> p (n t)"))
                    done = JB * (jb + 1)
            h_codes.append(codes)
            h_scales.append(scales)

        out_view = out.rearrange("(mt p) j -> p mt j", p=P)

        def match(n, bank, mt0, tiles, j0, width, result):
            e = psum.tile([P, tiles, width], F32, name=f"e{n}", tag=f"bank{bank}")
            jc = slice(j0, j0 + width)
            for u in range(tiles):
                g, r = divmod(mt0 + u, 4)
                cols = slice(P * r, P * (r + 1))
                for b in range(2):
                    nc.tensor.matmul_mx(
                        out=e[:, u, :], lhsT=v2_words[b, g][:, cols].bitcast(FP8X4), lhsT_scale=v2_scales[g][4 * b :, cols],
                        rhs=h_codes[b][:, jc].bitcast(FP8X4), rhs_scale=h_scales[b][:, jc], start=(b == 0), stop=(b == 1),
                    )
            bounded = sb(f"bounded{n}", [P, tiles, width], F32)
            weighted = sb(f"weighted{n}", [P, tiles, width], F32)
            nc.vector.tensor_tensor(out=weighted[:], in0=e[:], in1=prior_sb[j0 // JH][:, mt0 : mt0 + tiles, j0 % JH : j0 % JH + width], op=ALU.mult)
            nc.scalar.activation(out=bounded[:], in_=e[:], func=ACT.Tanh)
            adder = nc.gpsimd if n < GP_ADDS else nc.vector
            adder.tensor_tensor(out=result, in0=bounded[:], in1=weighted[:], op=ALU.add)

        for g in range(2):
            result = sb(f"result_first{g}", [P, 4, JH], F32)
            for jb in range(2):
                n = 2 * g + jb
                match(n, 2 * n, 4 * g, 4, JB * jb, JB, result[:, :, JB * jb : JB * (jb + 1)])
            nc.sync.dma_start(out=out_view[:, 4 * g : 4 * g + 4, :JH], in_=result[:])
        for mp in range(4):
            result = sb(f"result_second{mp}", [P, 2, JH], F32)
            match(4 + mp, 2 * mp + 1, 2 * mp, 2, JH, JH, result[:])
            nc.sync.dma_start(out=out_view[:, 2 * mp : 2 * mp + 2, JH:], in_=result[:])
